import numpy as np, ml_dtypes
CORES = [43,35,59,51,47,39,63,55]
N = 8
G1 = [0,1,2,3,4,5,6,7]
G2 = [7,6,5,4,3,2,1,0]
ROOT2 = 6
G3 = [0,2,4,6]
def setup_inputs(rng):
    return {"x1": rng.standard_normal((N, 128, 64), dtype=np.float32).astype(ml_dtypes.bfloat16), "x2": rng.standard_normal((N, 128, 256), dtype=np.float32), "x3": rng.standard_normal((N, 128, 4), dtype=np.float32)}
def reference(x1, x2, x3):
    out = {}
    y = np.full((N, 128, 512), np.nan, x1.dtype)
    s = np.concatenate([x1[r] for r in G1], axis=1)
    for r in G1:
        y[r] = s
    out["y1"] = y
    y = np.full((N, 128, 256), np.nan, x2.dtype)
    y[G2[ROOT2]] = x2[G2].sum(axis=0, dtype=np.float64).astype(x2.dtype)
    out["y2"] = y
    y = np.full((N, 128, 4), np.nan, x3.dtype)
    for i, r in enumerate(G3):
        y[G3[(i + 1) % 4]] = x3[r]
    out["y3"] = y
    return out

@@ -1,0 +1,131 @@
+from concourse.bass import DstId, RemoteDMATransfer
+
+NQ = 4
+
+SCRATCH = {
+    "d1": ("dram", [8, 128, 64], "bfloat16"),
+    "d2src": ("dram", [NQ, 128, 64], "float32"),
+    "d2land": ("dram", [8, 128, 64], "float32"),
+    "d2res": ("dram", [NQ, 128, 64], "float32"),
+    "d3src": ("dram", [128, 4], "float32"),
+    "d3land": ("dram", [128, 4], "float32"),
+}
+SEMAPHORES = ["ld1", "ld2", "ld3", "sent", "r2arr", "r2res", "s3arr", "st"] + ["a1_%d" % j for j in range(8)]
+
+
+def _bits(m):
+    return [b for b in range(m.bit_length()) if (m >> b) & 1]
+
+
+def _split(m, k):
+    bits = _bits(m)
+    n = len(bits) // k
+    return [sum(1 << b for b in bits[i * n:(i + 1) * n]) for i in range(k)]
+
+
+def _dst(topo, c):
+    rid, pid, _se = topo.addr(c)
+    return DstId(rid=rid, pnc=pid)
+
+
+def _hops(topo, a, b):
+    ca, cb = topo.chip(a), topo.chip(b)
+    if ca == cb:
+        return 0
+    return 1 if (topo.mates(ca, cb) or topo.same_plane(ca, cb)) else 2
+
+
+def rank_program(g, core, T, topo):
+    tb = T.tables
+    G1, G2, G3, ROOT2 = tb["G1"], tb["G2"], tb["G3"], tb["ROOT2"]
+    cores = list(T.cores)
+    S = T.sem
+    root = cores[G2[ROOT2]]
+    free = [c for c in range(topo.CORES_PER_CHIP * topo.CHIPS)
+            if topo.chip(c) == topo.chip(root) and T.rank_of(c) is None]
+    free.sort(key=lambda c: (topo.die(c) != topo.die(root), c))
+    folders = free[:NQ]
+    rank = T.rank_of(core)
+
+    if rank is None:
+        if core not in folders:
+            return
+        q = folders.index(core)
+        need = sum(len(_bits(topo.mask(cores[r], core))) // NQ for r in G2)
+        m = topo.mask(core, root)
+        g.wait_ge(S.r2arr, need)
+        g.remote_dma_fused([RemoteDMATransfer(
+            dst_ids=[_dst(topo, root)], dma_engine_mask=m, remote_sem=S.r2res,
+            srcs=[T.d2land[k] for k in range(len(G2))], dsts=[T.d2res[q]], alu_op=1)], local_sem=S.sent)
+        g.wait_ge(S.sent, len(_bits(m)))
+        return
+
+    sent = 0
+    stores = 0
+    m1 = G1.index(rank)
+    m2 = G2.index(rank)
+    in3 = rank in G3
+
+    g.sync.dma_start(T.d2src[:], T.x2[:]).then_inc(S.ld2, 16)
+    g.scalar.dma_start(T.d1[m1], T.x1[:]).then_inc(S.ld1, 16)
+    if in3:
+        g.scalar.dma_start(T.d3src[:], T.x3[:]).then_inc(S.ld3, 16)
+    g.scalar.dma_start(T.y1[:, m1 * 64:(m1 + 1) * 64], T.x1[:]).then_inc(S.st, 16)
+    stores += 16
+
+    masks = _split(topo.mask(core, folders[0]), NQ)
+    g.wait_ge(S.ld2, 16)
+    g.remote_dma_fused([RemoteDMATransfer(
+        dst_ids=[_dst(topo, folders[q])], dma_engine_mask=masks[q], remote_sem=S.r2arr,
+        src=T.d2src[q], dst=T.d2land[m2]) for q in range(NQ)], local_sem=S.sent)
+    sent += sum(len(_bits(x)) for x in masks)
+
+    others = [cores[r] for r in G1 if r != rank]
+    off = sorted([c for c in others if topo.chip(c) != topo.chip(core)], key=lambda c: -_hops(topo, core, c))
+    on = [c for c in others if topo.chip(c) == topo.chip(core)]
+    m_off = topo.mask(core, off[0])
+    for c in off:
+        m_off &= topo.mask(core, c)
+    m_on = topo.mask(core, on[0]) & ~m_off
+    my_sem = S["a1_%d" % m1]
+    g.wait_ge(S.ld1, 16)
+    g.remote_dma_fused([
+        RemoteDMATransfer(dst_ids=[_dst(topo, c) for c in off], dma_engine_mask=m_off, remote_sem=my_sem,
+                          srcs=[T.d1[m1]], dsts=[T.d1[m1] for _c in off]),
+        RemoteDMATransfer(dst_ids=[_dst(topo, c) for c in on], dma_engine_mask=m_on, remote_sem=my_sem,
+                          srcs=[T.d1[m1]], dsts=[T.d1[m1] for _c in on]),
+    ], local_sem=S.sent)
+    sent += len(_bits(m_off)) + len(_bits(m_on))
+
+    if in3:
+        nxt = cores[G3[(G3.index(rank) + 1) % len(G3)]]
+        prv = cores[G3[(G3.index(rank) - 1) % len(G3)]]
+        rid, pid, _se = topo.addr(nxt)
+        m3 = topo.mask(core, nxt)
+        g.wait_ge(S.ld3, 16)
+        g.remote_dma(T.d3land[:], T.d3src[:], S.s3arr, S.sent, pid, rid, m3)
+        sent += len(_bits(m3))
+
+    srcs = sorted([m for m, r in enumerate(G1) if r != rank], key=lambda m: (_hops(topo, cores[G1[m]], core), m))
+    if core == root:
+        share = [srcs[:3], srcs[3:]]
+    else:
+        share = [srcs[1::2], srcs[0::2]]
+    for qu, lst in ((g.sync, share[0]), (g.scalar, share[1])):
+        for m in lst:
+            c = cores[G1[m]]
+            n = len(_bits(m_on)) if topo.chip(c) == topo.chip(core) else len(_bits(topo.mask(c, core)))
+            qu.wait_ge(S["a1_%d" % m], n)
+            qu.dma_start(T.y1[:, m * 64:(m + 1) * 64], T.d1[m]).then_inc(S.st, 16)
+            stores += 16
+    if in3:
+        g.sync.wait_ge(S.s3arr, len(_bits(topo.mask(prv, core))))
+        g.sync.dma_start(T.y3[:], T.d3land[:]).then_inc(S.st, 16)
+        stores += 16
+    if core == root:
+        g.sync.wait_ge(S.r2res, sum(len(_bits(topo.mask(f, root))) for f in folders))
+        g.sync.dma_start(T.y2[:], T.d2res[:]).then_inc(S.st, 16)
+        stores += 16
+
+    g.wait_ge(S.sent, sent)
+    g.wait_ge(S.st, stores)

@@ -1,12 +1,12 @@
 from concourse.bass import DstId, RemoteDMATransfer
 
-NQ = 4
+NP = 8
 
 SCRATCH = {
     "d1": ("dram", [8, 128, 64], "bfloat16"),
-    "d2src": ("dram", [NQ, 128, 64], "float32"),
-    "d2land": ("dram", [8, 128, 64], "float32"),
-    "d2res": ("dram", [NQ, 128, 64], "float32"),
+    "d2src": ("dram", [NP, 128, 32], "float32"),
+    "d2land": ("dram", [8, 128, 32], "float32"),
+    "d2res": ("dram", [NP, 128, 32], "float32"),
     "d3src": ("dram", [128, 4], "float32"),
     "d3land": ("dram", [128, 4], "float32"),
 }
@@ -15,12 +15,6 @@ SEMAPHORES = ["ld1", "ld2", "ld3", "sent", "r2arr", "r2res", "s3arr", "st"] + ["
 
 def _bits(m):
     return [b for b in range(m.bit_length()) if (m >> b) & 1]
-
-
-def _split(m, k):
-    bits = _bits(m)
-    n = len(bits) // k
-    return [sum(1 << b for b in bits[i * n:(i + 1) * n]) for i in range(k)]
 
 
 def _dst(topo, c):
@@ -41,22 +35,23 @@ def rank_program(g, core, T, topo):
     cores = list(T.cores)
     S = T.sem
     root = cores[G2[ROOT2]]
-    free = [c for c in range(topo.CORES_PER_CHIP * topo.CHIPS)
-            if topo.chip(c) == topo.chip(root) and T.rank_of(c) is None]
-    free.sort(key=lambda c: (topo.die(c) != topo.die(root), c))
-    folders = free[:NQ]
+    places = sorted(set((topo.chip(c), topo.die(c)) for c in cores))
+    folders = []
+    for ch, di in places:
+        folders.append([c for c in range(topo.CORES_PER_CHIP * topo.CHIPS)
+                        if topo.chip(c) == ch and topo.die(c) == di and T.rank_of(c) is None
+                        and topo.may_write(c, root)][0])
     rank = T.rank_of(core)
 
     if rank is None:
         if core not in folders:
             return
-        q = folders.index(core)
-        need = sum(len(_bits(topo.mask(cores[r], core))) // NQ for r in G2)
+        p = folders.index(core)
         m = topo.mask(core, root)
-        g.wait_ge(S.r2arr, need)
+        g.wait_ge(S.r2arr, len(G2))
         g.remote_dma_fused([RemoteDMATransfer(
             dst_ids=[_dst(topo, root)], dma_engine_mask=m, remote_sem=S.r2res,
-            srcs=[T.d2land[k] for k in range(len(G2))], dsts=[T.d2res[q]], alu_op=1)], local_sem=S.sent)
+            srcs=[T.d2land[k] for k in range(len(G2))], dsts=[T.d2res[p]], alu_op=1)], local_sem=S.sent)
         g.wait_ge(S.sent, len(_bits(m)))
         return
 
@@ -73,13 +68,6 @@ def rank_program(g, core, T, topo):
     g.scalar.dma_start(T.y1[:, m1 * 64:(m1 + 1) * 64], T.x1[:]).then_inc(S.st, 16)
     stores += 16
 
-    masks = _split(topo.mask(core, folders[0]), NQ)
-    g.wait_ge(S.ld2, 16)
-    g.remote_dma_fused([RemoteDMATransfer(
-        dst_ids=[_dst(topo, folders[q])], dma_engine_mask=masks[q], remote_sem=S.r2arr,
-        src=T.d2src[q], dst=T.d2land[m2]) for q in range(NQ)], local_sem=S.sent)
-    sent += sum(len(_bits(x)) for x in masks)
-
     others = [cores[r] for r in G1 if r != rank]
     off = sorted([c for c in others if topo.chip(c) != topo.chip(core)], key=lambda c: -_hops(topo, core, c))
     on = [c for c in others if topo.chip(c) == topo.chip(core)]
@@ -87,6 +75,17 @@ def rank_program(g, core, T, topo):
     for c in off:
         m_off &= topo.mask(core, c)
     m_on = topo.mask(core, on[0]) & ~m_off
+
+    e_off, e_on = _bits(m_off), _bits(m_on)
+    trs = []
+    for p, f in enumerate(folders):
+        e = e_on.pop(0) if topo.chip(f) == topo.chip(core) else e_off.pop(0)
+        trs.append(RemoteDMATransfer(dst_ids=[_dst(topo, f)], dma_engine_mask=1 << e, remote_sem=S.r2arr,
+                                     src=T.d2src[p], dst=T.d2land[m2]))
+    g.wait_ge(S.ld2, 16)
+    g.remote_dma_fused(trs, local_sem=S.sent)
+    sent += len(trs)
+
     my_sem = S["a1_%d" % m1]
     g.wait_ge(S.ld1, 16)
     g.remote_dma_fused([

@@ -10,7 +10,8 @@ SCRATCH = {
     "d3src": ("dram", [128, 4], "float32"),
     "d3land": ("dram", [128, 4], "float32"),
 }
-SEMAPHORES = ["ld1", "ld2", "ld3", "sent", "r2arr", "r2res", "s3arr", "st"] + ["a1_%d" % j for j in range(8)]
+SEMAPHORES = (["ld1", "ld2", "ld3", "sent", "r2arr", "s3arr", "st"] + ["r2res%d" % h for h in range(3)]
+              + ["a1_%d" % j for j in range(8)])
 
 
 def _bits(m):
@@ -26,7 +27,29 @@ def _hops(topo, a, b):
     ca, cb = topo.chip(a), topo.chip(b)
     if ca == cb:
         return 0
-    return 1 if (topo.mates(ca, cb) or topo.same_plane(ca, cb)) else 2
+    return 1 if (topo.mask(a, b) and (topo.mates(ca, cb) or topo.same_plane(ca, cb))) else 2
+
+
+def _engines(topo, src, dsts):
+    m_off = m_all = 0
+    for c in dsts:
+        if topo.chip(c) == topo.chip(src):
+            m_all = topo.mask(src, c)
+        else:
+            m_off = topo.mask(src, c) if not m_off else m_off & topo.mask(src, c)
+    return m_off, m_all & ~m_off
+
+
+def _piece_masks(topo, src, folders):
+    m_off, m_on = _engines(topo, src, folders)
+    e_off, e_on = _bits(m_off), _bits(m_on)
+    masks = [0] * len(folders)
+    for p, f in enumerate(folders):
+        masks[p] = 1 << (e_on.pop(0) if topo.chip(f) == topo.chip(src) else e_off.pop(0))
+    for p in sorted(range(len(folders)), key=lambda p: -_hops(topo, src, folders[p])):
+        if e_off and topo.chip(folders[p]) != topo.chip(src):
+            masks[p] |= 1 << e_off.pop(0)
+    return masks
 
 
 def rank_program(g, core, T, topo):
@@ -41,6 +64,7 @@ def rank_program(g, core, T, topo):
         folders.append([c for c in range(topo.CORES_PER_CHIP * topo.CHIPS)
                         if topo.chip(c) == ch and topo.die(c) == di and T.rank_of(c) is None
                         and topo.may_write(c, root)][0])
+    folders.sort(key=lambda c: (_hops(topo, c, root), c))
     rank = T.rank_of(core)
 
     if rank is None:
@@ -48,9 +72,9 @@ def rank_program(g, core, T, topo):
             return
         p = folders.index(core)
         m = topo.mask(core, root)
-        g.wait_ge(S.r2arr, len(G2))
+        g.wait_ge(S.r2arr, sum(len(_bits(_piece_masks(topo, cores[r], folders)[p])) for r in G2))
         g.remote_dma_fused([RemoteDMATransfer(
-            dst_ids=[_dst(topo, root)], dma_engine_mask=m, remote_sem=S.r2res,
+            dst_ids=[_dst(topo, root)], dma_engine_mask=m, remote_sem=S["r2res%d" % _hops(topo, core, root)],
             srcs=[T.d2land[k] for k in range(len(G2))], dsts=[T.d2res[p]], alu_op=1)], local_sem=S.sent)
         g.wait_ge(S.sent, len(_bits(m)))
         return
@@ -65,27 +89,21 @@ def rank_program(g, core, T, topo):
     g.scalar.dma_start(T.d1[m1], T.x1[:]).then_inc(S.ld1, 16)
     if in3:
         g.scalar.dma_start(T.d3src[:], T.x3[:]).then_inc(S.ld3, 16)
+    g.scalar.wait_ge(S.ld2, 16)
     g.scalar.dma_start(T.y1[:, m1 * 64:(m1 + 1) * 64], T.x1[:]).then_inc(S.st, 16)
     stores += 16
+
+    masks = _piece_masks(topo, core, folders)
+    g.wait_ge(S.ld2, 16)
+    g.remote_dma_fused([RemoteDMATransfer(
+        dst_ids=[_dst(topo, f)], dma_engine_mask=masks[p], remote_sem=S.r2arr,
+        src=T.d2src[p], dst=T.d2land[m2]) for p, f in enumerate(folders)], local_sem=S.sent)
+    sent += sum(len(_bits(x)) for x in masks)
 
     others = [cores[r] for r in G1 if r != rank]
     off = sorted([c for c in others if topo.chip(c) != topo.chip(core)], key=lambda c: -_hops(topo, core, c))
     on = [c for c in others if topo.chip(c) == topo.chip(core)]
-    m_off = topo.mask(core, off[0])
-    for c in off:
-        m_off &= topo.mask(core, c)
-    m_on = topo.mask(core, on[0]) & ~m_off
-
-    e_off, e_on = _bits(m_off), _bits(m_on)
-    trs = []
-    for p, f in enumerate(folders):
-        e = e_on.pop(0) if topo.chip(f) == topo.chip(core) else e_off.pop(0)
-        trs.append(RemoteDMATransfer(dst_ids=[_dst(topo, f)], dma_engine_mask=1 << e, remote_sem=S.r2arr,
-                                     src=T.d2src[p], dst=T.d2land[m2]))
-    g.wait_ge(S.ld2, 16)
-    g.remote_dma_fused(trs, local_sem=S.sent)
-    sent += len(trs)
-
+    m_off, m_on = _engines(topo, core, others)
     my_sem = S["a1_%d" % m1]
     g.wait_ge(S.ld1, 16)
     g.remote_dma_fused([
@@ -112,8 +130,7 @@ def rank_program(g, core, T, topo):
         share = [srcs[1::2], srcs[0::2]]
     for qu, lst in ((g.sync, share[0]), (g.scalar, share[1])):
         for m in lst:
-            c = cores[G1[m]]
-            n = len(_bits(m_on)) if topo.chip(c) == topo.chip(core) else len(_bits(topo.mask(c, core)))
+            n = len(_bits(m_on if topo.chip(cores[G1[m]]) == topo.chip(core) else m_off))
             qu.wait_ge(S["a1_%d" % m], n)
             qu.dma_start(T.y1[:, m * 64:(m + 1) * 64], T.d1[m]).then_inc(S.st, 16)
             stores += 16
@@ -122,9 +139,15 @@ def rank_program(g, core, T, topo):
         g.sync.dma_start(T.y3[:], T.d3land[:]).then_inc(S.st, 16)
         stores += 16
     if core == root:
-        g.sync.wait_ge(S.r2res, sum(len(_bits(topo.mask(f, root))) for f in folders))
-        g.sync.dma_start(T.y2[:], T.d2res[:]).then_inc(S.st, 16)
-        stores += 16
+        rows = 128 // NP
+        for h in range(3):
+            ps = [p for p, f in enumerate(folders) if _hops(topo, f, root) == h]
+            if not ps:
+                continue
+            g.sync.wait_ge(S["r2res%d" % h], sum(len(_bits(topo.mask(folders[p], root))) for p in ps))
+            g.sync.dma_start(T.y2[ps[0] * rows:(ps[-1] + 1) * rows, :],
+                             T.d2res[ps[0]:ps[-1] + 1]).then_inc(S.st, 16)
+            stores += 16
 
     g.wait_ge(S.sent, sent)
     g.wait_ge(S.st, stores)

@@ -27,7 +27,7 @@ def _hops(topo, a, b):
     ca, cb = topo.chip(a), topo.chip(b)
     if ca == cb:
         return 0
-    return 1 if (topo.mask(a, b) and (topo.mates(ca, cb) or topo.same_plane(ca, cb))) else 2
+    return 1 if (topo.mates(ca, cb) or topo.same_plane(ca, cb)) else 2
 
 
 def _engines(topo, src, dsts):
@@ -58,12 +58,15 @@ def rank_program(g, core, T, topo):
     cores = list(T.cores)
     S = T.sem
     root = cores[G2[ROOT2]]
-    places = sorted(set((topo.chip(c), topo.die(c)) for c in cores))
-    folders = []
-    for ch, di in places:
-        folders.append([c for c in range(topo.CORES_PER_CHIP * topo.CHIPS)
-                        if topo.chip(c) == ch and topo.die(c) == di and T.rank_of(c) is None
-                        and topo.may_write(c, root)][0])
+    idle = [c for c in range(topo.CORES_PER_CHIP * topo.CHIPS) if T.rank_of(c) is None and topo.may_write(c, root)]
+    places = sorted(set((topo.chip(c), topo.die(c)) for c in cores if _hops(topo, c, root) <= 1))
+    folders = [[c for c in idle if topo.chip(c) == ch and topo.die(c) == di][0] for ch, di in places]
+    home = [[c for c in idle if topo.chip(c) == ch and topo.die(c) == di and c not in folders]
+            for ch, di in places if ch == topo.chip(root)]
+    while len(folders) < NP:
+        for lst in home:
+            if lst and len(folders) < NP:
+                folders.append(lst.pop(0))
     folders.sort(key=lambda c: (_hops(topo, c, root), c))
     rank = T.rank_of(core)
 
@@ -86,9 +89,9 @@ def rank_program(g, core, T, topo):
     in3 = rank in G3
 
     g.sync.dma_start(T.d2src[:], T.x2[:]).then_inc(S.ld2, 16)
-    g.scalar.dma_start(T.d1[m1], T.x1[:]).then_inc(S.ld1, 16)
+    g.sync.dma_start(T.d1[m1], T.x1[:]).then_inc(S.ld1, 16)
     if in3:
-        g.scalar.dma_start(T.d3src[:], T.x3[:]).then_inc(S.ld3, 16)
+        g.sync.dma_start(T.d3src[:], T.x3[:]).then_inc(S.ld3, 16)
     g.scalar.wait_ge(S.ld2, 16)
     g.scalar.dma_start(T.y1[:, m1 * 64:(m1 + 1) * 64], T.x1[:]).then_inc(S.st, 16)
     stores += 16

from concourse.bass import DstId, RemoteDMATransfer

NP = 8

SCRATCH = {
    "d1": ("dram", [8, 128, 64], "bfloat16"),
    "d2src": ("dram", [NP, 128, 32], "float32"),
    "d2land": ("dram", [8, 128, 32], "float32"),
    "d2res": ("dram", [NP, 128, 32], "float32"),
    "d3src": ("dram", [128, 4], "float32"),
    "d3land": ("dram", [128, 4], "float32"),
}
SEMAPHORES = (["ld1", "ld2", "ld3", "sent", "r2arr", "s3arr", "st"] + ["r2res%d" % h for h in range(3)]
              + ["a1_%d" % j for j in range(8)])


def _bits(m):
    return [b for b in range(m.bit_length()) if (m >> b) & 1]


def _dst(topo, c):
    rid, pid, _se = topo.addr(c)
    return DstId(rid=rid, pnc=pid)


def _hops(topo, a, b):
    ca, cb = topo.chip(a), topo.chip(b)
    if ca == cb:
        return 0
    return 1 if (topo.mates(ca, cb) or topo.same_plane(ca, cb)) else 2


def _engines(topo, src, dsts):
    m_off = m_all = 0
    for c in dsts:
        if topo.chip(c) == topo.chip(src):
            m_all = topo.mask(src, c)
        else:
            m_off = topo.mask(src, c) if not m_off else m_off & topo.mask(src, c)
    return m_off, m_all & ~m_off


def _piece_masks(topo, src, folders):
    m_off, m_on = _engines(topo, src, folders)
    e_off, e_on = _bits(m_off), _bits(m_on)
    masks = [0] * len(folders)
    for p, f in enumerate(folders):
        masks[p] = 1 << (e_on.pop(0) if topo.chip(f) == topo.chip(src) else e_off.pop(0))
    for p in sorted(range(len(folders)), key=lambda p: -_hops(topo, src, folders[p])):
        if e_off and topo.chip(folders[p]) != topo.chip(src):
            masks[p] |= 1 << e_off.pop(0)
    return masks


def rank_program(g, core, T, topo):
    tb = T.tables
    G1, G2, G3, ROOT2 = tb["G1"], tb["G2"], tb["G3"], tb["ROOT2"]
    cores = list(T.cores)
    S = T.sem
    root = cores[G2[ROOT2]]
    idle = [c for c in range(topo.CORES_PER_CHIP * topo.CHIPS) if T.rank_of(c) is None and topo.may_write(c, root)]
    places = sorted(set((topo.chip(c), topo.die(c)) for c in cores if _hops(topo, c, root) <= 1))
    folders = [[c for c in idle if topo.chip(c) == ch and topo.die(c) == di][0] for ch, di in places]
    home = [[c for c in idle if topo.chip(c) == ch and topo.die(c) == di and c not in folders]
            for ch, di in places if ch == topo.chip(root)]
    while len(folders) < NP:
        for lst in home:
            if lst and len(folders) < NP:
                folders.append(lst.pop(0))
    folders.sort(key=lambda c: (_hops(topo, c, root), c))
    rank = T.rank_of(core)

    if rank is None:
        if core not in folders:
            return
        p = folders.index(core)
        m = topo.mask(core, root)
        g.wait_ge(S.r2arr, sum(len(_bits(_piece_masks(topo, cores[r], folders)[p])) for r in G2))
        g.remote_dma_fused([RemoteDMATransfer(
            dst_ids=[_dst(topo, root)], dma_engine_mask=m, remote_sem=S["r2res%d" % _hops(topo, core, root)],
            srcs=[T.d2land[k] for k in range(len(G2))], dsts=[T.d2res[p]], alu_op=1)], local_sem=S.sent)
        g.wait_ge(S.sent, len(_bits(m)))
        return

    sent = 0
    stores = 0
    m1 = G1.index(rank)
    m2 = G2.index(rank)
    in3 = rank in G3

    g.sync.dma_start(T.d2src[:], T.x2[:]).then_inc(S.ld2, 16)
    g.sync.dma_start(T.d1[m1], T.x1[:]).then_inc(S.ld1, 16)
    if in3:
        g.sync.dma_start(T.d3src[:], T.x3[:]).then_inc(S.ld3, 16)
    g.scalar.wait_ge(S.ld2, 16)
    g.scalar.dma_start(T.y1[:, m1 * 64:(m1 + 1) * 64], T.x1[:]).then_inc(S.st, 16)
    stores += 16

    masks = _piece_masks(topo, core, folders)
    g.wait_ge(S.ld2, 16)
    g.remote_dma_fused([RemoteDMATransfer(
        dst_ids=[_dst(topo, f)], dma_engine_mask=masks[p], remote_sem=S.r2arr,
        src=T.d2src[p], dst=T.d2land[m2]) for p, f in enumerate(folders)], local_sem=S.sent)
    sent += sum(len(_bits(x)) for x in masks)

    others = [cores[r] for r in G1 if r != rank]
    off = sorted([c for c in others if topo.chip(c) != topo.chip(core)], key=lambda c: -_hops(topo, core, c))
    on = [c for c in others if topo.chip(c) == topo.chip(core)]
    m_off, m_on = _engines(topo, core, others)
    my_sem = S["a1_%d" % m1]
    g.wait_ge(S.ld1, 16)
    g.remote_dma_fused([
        RemoteDMATransfer(dst_ids=[_dst(topo, c) for c in off], dma_engine_mask=m_off, remote_sem=my_sem,
                          srcs=[T.d1[m1]], dsts=[T.d1[m1] for _c in off]),
        RemoteDMATransfer(dst_ids=[_dst(topo, c) for c in on], dma_engine_mask=m_on, remote_sem=my_sem,
                          srcs=[T.d1[m1]], dsts=[T.d1[m1] for _c in on]),
    ], local_sem=S.sent)
    sent += len(_bits(m_off)) + len(_bits(m_on))

    if in3:
        nxt = cores[G3[(G3.index(rank) + 1) % len(G3)]]
        prv = cores[G3[(G3.index(rank) - 1) % len(G3)]]
        rid, pid, _se = topo.addr(nxt)
        m3 = topo.mask(core, nxt)
        g.wait_ge(S.ld3, 16)
        g.remote_dma(T.d3land[:], T.d3src[:], S.s3arr, S.sent, pid, rid, m3)
        sent += len(_bits(m3))

    srcs = sorted([m for m, r in enumerate(G1) if r != rank], key=lambda m: (_hops(topo, cores[G1[m]], core), m))
    if core == root:
        share = [srcs[:3], srcs[3:]]
    else:
        share = [srcs[1::2], srcs[0::2]]
    for qu, lst in ((g.sync, share[0]), (g.scalar, share[1])):
        for m in lst:
            n = len(_bits(m_on if topo.chip(cores[G1[m]]) == topo.chip(core) else m_off))
            qu.wait_ge(S["a1_%d" % m], n)
            qu.dma_start(T.y1[:, m * 64:(m + 1) * 64], T.d1[m]).then_inc(S.st, 16)
            stores += 16
    if in3:
        g.sync.wait_ge(S.s3arr, len(_bits(topo.mask(prv, core))))
        g.sync.dma_start(T.y3[:], T.d3land[:]).then_inc(S.st, 16)
        stores += 16
    if core == root:
        rows = 128 // NP
        for h in range(3):
            ps = [p for p, f in enumerate(folders) if _hops(topo, f, root) == h]
            if not ps:
                continue
            g.sync.wait_ge(S["r2res%d" % h], sum(len(_bits(topo.mask(folders[p], root))) for p in ps))
            g.sync.dma_start(T.y2[ps[0] * rows:(ps[-1] + 1) * rows, :],
                             T.d2res[ps[0]:ps[-1] + 1]).then_inc(S.st, 16)
            stores += 16

    g.wait_ge(S.sent, sent)
    g.wait_ge(S.st, stores)
